import numpy as np, ml_dtypes
CORES = [26,28,98,100,106,108,122,124]
N = 8
import mx_ref
NC, KT, ROOT = 128, 1, 1
BF = ml_dtypes.bfloat16
def cut(t, i, w=512):
    return t[:, w * i:w * i + w]
def pk(c, s, i=0):
    return (np.ascontiguousarray(c[:, 512 * i:512 * i + 512]), mx_ref.live(s[:, 128 * i:128 * i + 128]))
def inputs(rng, e, E):
    def f(*shape):
        v = (rng.standard_normal(shape, dtype=np.float32) * np.exp2(rng.integers(-2, 3, shape[:-1] + (1,)))).astype(BF)
        return mx_ref.spread((v.astype(np.float32) * np.exp2(rng.integers(-E, E + 1, shape[:-2] + (1, 1))).astype(np.float32)).astype(BF), rng, e)
    def packed(k):
        c = np.zeros((N, 128, k * 512), np.uint8); s = np.zeros((N, 128, k * 128), np.uint8)
        for r in range(N):
            for i in range(k):
                a, b = mx_ref.quantize(f(128, 512)); c[r][:, 512 * i:512 * i + 512] = a; s[r][:, 128 * i:128 * i + 128] = mx_ref.plane(b, rng)
        return c, s
    d = {}
    d["wc"], d["ws"] = packed(KT)
    d["x"] = f(N, 128, KT * 4 * NC)
    return d
def setup_inputs(rng):
    return inputs(rng, 0, 0)
def setup_inputs_blocks(rng):
    return inputs(rng, 4, 0)
def setup_inputs_wide(rng):
    return inputs(rng, 0, 8)
def reference(wc, ws, x):
    y = np.zeros((N, 128, NC), np.float32)
    for r in range(N):
        for t in range(KT):
            p = mx_ref.matmul(pk(wc[ROOT], ws[ROOT], t), mx_ref.quantize(cut(x[r], t, 4 * NC)))
            y[r] = p if t == 0 else y[r] + p
    return {"y": y}

from concourse.bass import DstId, RemoteDMATransfer
from concourse.mybir import dt

SCRATCH = {
    "wq": ("sbuf", [128, 128], "float8_e4m3fn_x4"),
    "wp": ("sbuf", [128, 128], "uint8"),
    "wqd": ("dram", [128, 128], "float8_e4m3fn_x4"),
    "wpd": ("dram", [128, 128], "uint8"),
    "xb": ("sbuf", [128, 512], "bfloat16"),
    "xq": ("sbuf", [128, 128], "float8_e4m3fn_x4"),
    "xp": ("sbuf", [128, 128], "uint8"),
    "acc": ("psum", [128, 512], "float32"),
    "yo": ("sbuf", [128, 128], "float32"),
}
SEMAPHORES = ["ldp", "ldc", "own", "xin", "xqd", "pl", "cd", "sent", "mm", "cp", "out"]

K_PLANE = 8
K_CODES = 16
K_CARRY = 8


def _pick(mask, k):
    bits = [b for b in range(mask.bit_length()) if (mask >> b) & 1]
    k = min(k, len(bits))
    m = 0
    for b in bits[::len(bits) // k][:k]:
        m |= 1 << b
    return m, k


def _plan(T, topo):
    root = T.cores[T.root]
    home = topo.chip(root)
    near = [c for c in T.cores if c != root and topo.chip(c) == home]
    far = [c for c in T.cores if topo.chip(c) != home]
    spare = [c for c in range(topo.CHIPS * topo.CORES_PER_CHIP) if topo.chip(c) == home and c not in T.cores]
    far.sort(key=lambda d: sum(1 for h in spare if topo.may_write(h, d)))
    carrier = {}
    for d in far:
        ok = [h for h in spare if h not in carrier.values() and topo.may_write(h, d)]
        ok.sort(key=lambda h: topo.die(h) != topo.die(d))
        carrier[d] = ok[0]
    return root, near, carrier


def _fan(g, topo, me, dests, src, dst, k, sem, local):
    mask = topo.mask(me, dests[0])
    for d in dests:
        mask &= topo.mask(me, d)
    m, k = _pick(mask, k)
    ids = [DstId(rid=topo.addr(d)[0], pnc=topo.addr(d)[1]) for d in dests]
    g.remote_dma_fused([RemoteDMATransfer(dst_ids=ids, dma_engine_mask=m, remote_sem=sem, srcs=[src],
                                          dsts=[dst for _ in dests])], local_sem=local)
    return k


def rank_program(g, core, T, topo):
    S = T.sem
    u8 = dt.uint8
    root, near, carrier = _plan(T, topo)
    rank = T.rank_of(core)
    hands = list(carrier.values())
    k_plane = _pick(topo.mask(root, hands[0]), K_PLANE)[1]
    k_codes = _pick(topo.mask(root, hands[0]), K_CODES)[1]

    if core in hands:
        d = [r for r in carrier if carrier[r] == core][0]
        g.wait_ge(S.pl, k_plane)
        n = _fan(g, topo, core, [d], T.wpd[:], T.wp[:], K_CARRY, S.pl, S.sent)
        g.wait_ge(S.cd, k_codes)
        n += _fan(g, topo, core, [d], T.wqd[:].bitcast(u8), T.wq[:].bitcast(u8), K_CARRY, S.cd, S.sent)
        g.wait_ge(S.sent, n)
        return
    if rank is None:
        return

    if core == root:
        g.sync.dma_start(T.wpd[:], T.ws[:]).then_inc(S.ldp, 16)
        g.scalar.dma_start(T.wqd[:].bitcast(u8), T.wc[:]).then_inc(S.ldc, 16)
        g.sync.dma_start(T.xb[:], T.x[:]).then_inc(S.xin, 16)
        g.scalar.dma_start(T.wq[:].bitcast(u8), T.wc[:]).then_inc(S.own, 16)
        g.sync.dma_start(T.wp[:], T.ws[:]).then_inc(S.own, 16)
    else:
        g.sync.dma_start(T.xb[:], T.x[:]).then_inc(S.xin, 16)

    if core == root:
        g.wait_ge(S.ldp, 16)
        n = _fan(g, topo, core, hands, T.wpd[:], T.wpd[:], K_PLANE, S.pl, S.sent)
        g.wait_ge(S.ldc, 16)
        n += _fan(g, topo, core, hands, T.wqd[:].bitcast(u8), T.wqd[:].bitcast(u8), K_CODES, S.cd, S.sent)
        if near:
            n += _fan(g, topo, core, near, T.wqd[:].bitcast(u8), T.wq[:].bitcast(u8), K_CODES, S.cd, S.sent)
            n += _fan(g, topo, core, near, T.wpd[:], T.wp[:], K_CODES, S.pl, S.sent)
        g.wait_ge(S.sent, n)

    g.vector.wait_ge(S.xin, 16)
    g.vector.quantize_mx(T.xq[:], T.xp[:], T.xb[:]).then_inc(S.xqd, 1)

    g.tensor.wait_ge(S.xqd, 1)
    if core == root:
        g.tensor.wait_ge(S.own, 32)
    elif core in near:
        g.tensor.wait_ge(S.pl, k_codes)
        g.tensor.wait_ge(S.cd, k_codes)
    else:
        k = _pick(topo.mask(carrier[core], core), K_CARRY)[1]
        g.tensor.wait_ge(S.pl, k)
        g.tensor.wait_ge(S.cd, k)
    g.tensor.matmul_mx(T.acc[:, 0:128], T.wq[:], T.wp[:], T.xq[:], T.xp[:], True, True).then_inc(S.mm, 1)
    g.vector.wait_ge(S.mm, 1)
    g.vector.tensor_copy(T.yo[:], T.acc[:, 0:128]).then_inc(S.cp, 1)
    g.sync.wait_ge(S.cp, 1)
    g.sync.dma_start(T.y[:], T.yo[:]).then_inc(S.out, 16)
    g.sync.wait_ge(S.out, 16)
